import numpy as np
import ml_dtypes


def mxq(x, axis, fmt="e4m3"):
    dtype, down = {"e4m3": (ml_dtypes.float8_e4m3fn, 7), "e5m2": (ml_dtypes.float8_e5m2, 14)}[fmt]
    v = np.moveaxis(np.asarray(x, np.float32).astype(ml_dtypes.bfloat16).astype(np.float64), axis, -1)
    blocks = v.reshape(v.shape[:-1] + (-1, 32))
    amax = np.abs(blocks).max(-1, keepdims=True)
    byte = np.maximum(np.where(amax > 0, np.frexp(amax)[1] - 1 + 127, 0) - down, 1)
    scale = np.exp2(byte - 127.0)
    codes = (blocks / scale).astype(np.float32).astype(dtype).astype(np.float64)
    return np.moveaxis((codes * scale).reshape(v.shape), -1, axis)


WIDE = False


def mx_kscale(k):
    if not WIDE:
        return np.ones(k)
    levels = np.array([10, -10, 5, -5, 0])
    if k % 512:
        return np.exp2(np.random.permutation(np.resize(levels, k // 32))).repeat(32)
    a = np.empty((k // 512, 16))
    for p in range(k // 512):
        a[p, :8] = np.random.permutation(np.resize(levels, 8))
        for g in range(8):
            far = levels[np.abs(levels - a[p, g]) >= 10]
            a[p, g + 8] = far[np.random.randint(len(far))]
    return np.exp2(a.ravel()).repeat(32)


def f64(x):
    return np.asarray(x).astype(np.float64)


def striped(idx):
    return np.tile(idx.reshape(-1, 16).T, (8, 1)).astype(np.uint16)


def unstriped(offs):
    return offs[:16].T.reshape(-1).astype(np.int64)


E2M1 = np.array([0.0, 0.5, 1.0, 1.5, 2.0, 3.0, 4.0, 6.0, -0.0, -0.5, -1.0, -1.5, -2.0, -3.0, -4.0, -6.0])


def pack_weight(w, fmt):
    k, n = w.shape
    w = f64(np.asarray(w, np.float32).astype(ml_dtypes.bfloat16)).reshape(k // 32, 32, n)
    amax = np.abs(w).max(1)
    if fmt == "e4m3":
        byte = np.frexp(amax)[1] - 1 + 127 - 7
    else:
        mant, ex = np.frexp(amax / 6.0)
        byte = np.where(mant > 0.5, ex, ex - 1) + 127
    byte = np.clip(np.where(amax > 0, byte, 1), 1, 254)
    scaled = (w * np.exp2(127.0 - byte)[:, None, :]).reshape(k, n).astype(np.float32)
    by_word = np.ascontiguousarray(scaled.reshape(k // 512, 128, 4, n).transpose(0, 1, 3, 2))
    if fmt == "e4m3":
        words = by_word.astype(ml_dtypes.float8_e4m3fn).view(np.uint8)
    else:
        c = by_word.astype(ml_dtypes.float4_e2m1fn).view(np.uint8) & 0xF
        words = (c[..., 0::2] | (c[..., 1::2] << 4)).reshape(k // 512, 128, 2 * n)
    return np.ascontiguousarray(words), np.ascontiguousarray(byte.astype(np.uint8).reshape(k // 512, 16, n))


def unpack_weight(words, scales, fmt):
    g, _, n = scales.shape
    words = np.ascontiguousarray(words).reshape(g, 128, n, -1)
    if fmt == "e4m3":
        vals = words.view(ml_dtypes.float8_e4m3fn).astype(np.float64)
    else:
        nib = np.empty((g, 128, n, 4), np.uint8)
        nib[..., 0::2] = words & 0xF
        nib[..., 1::2] = words >> 4
        vals = E2M1[nib]
    vals = vals * np.repeat(np.exp2(scales.astype(np.float64) - 127.0), 8, axis=1)[..., None]
    return vals.transpose(0, 1, 3, 2).reshape(g * 512, n)


def gelu(v):
    return 0.5 * v * (1.0 + np.tanh(np.sqrt(2.0 / np.pi) * (v + 0.044715 * v**3)))


K, H, T, S, P = 1536, 1024, 2048, 1024, 512

def setup_inputs():
    n = np.random.standard_normal
    s = mx_kscale(K)[:, None]
    u = mx_kscale(H)
    tab_words, tab_scales = pack_weight(n((K, T)) * s, "e4m3")
    w1_words, w1_scales = pack_weight(n((K, H)) / np.sqrt(K) / s, "e2m1")
    return {
        "tab_words": tab_words, "tab_scales": tab_scales,
        "offs": striped(np.random.permutation(T)[:S]),
        "w1_words": w1_words, "w1_scales": w1_scales,
        "pos1": striped(np.random.permutation(S)[:P]),
        "pos2": striped(np.random.permutation(S)[:P]),
        "gm": (np.exp(0.3 * n(H)) * u).astype(np.float32),
        "gv": (-np.exp(0.3 * n(H)) * u).astype(np.float32),
        "w2": (n((H, H)) / np.sqrt(H) / u[:, None]).astype(np.float32),
    }

def reference(tab_words, tab_scales, offs, w1_words, w1_scales, pos1, pos2, gm, gv, w2):
    v = unpack_weight(tab_words, tab_scales, "e4m3")[:, unstriped(offs)]
    w1 = unpack_weight(w1_words, w1_scales, "e2m1")
    h = w1.T @ v
    hm = h[:, unstriped(pos1)]
    hv = h[:, unstriped(pos2)]
    zm = mxq(f64(gm)[:, None] * np.tanh(hm), 0, "e4m3")
    zv = mxq(f64(gv)[:, None] * np.tanh(hv), 0, "e4m3")
    wq = mxq(f64(w2), 0, "e4m3")
    y = wq.T @ zm + wq.T @ zv
    return np.abs(y) * hv

@@ -1,0 +1,272 @@
+from contextlib import ExitStack
+
+import concourse.mybir as mybir
+from concourse.masks import make_identity
+
+K, H, T, S, M = 1536, 1024, 2048, 1024, 512
+FLOPS = 2 * K * H * S + 2 * 2 * H * H * M
+
+F32 = mybir.dt.float32
+BF16 = mybir.dt.bfloat16
+I32 = mybir.dt.int32
+U32 = mybir.dt.uint32
+U16 = mybir.dt.uint16
+U8 = mybir.dt.uint8
+FP8X4 = mybir.dt.float8_e4m3fn_x4
+FP4X4 = mybir.dt.float4_e2m1fn_x4
+ACT = mybir.ActivationFunctionType
+MULT = mybir.AluOpType.mult
+
+P = 128
+CHUNKS = [256,128,128]
+UNIT = 256
+
+
+def tile_list_crease_side_contrast_kernel(
+    tc, tab_words, tab_scales, offs, w1_words, w1_scales, pos1, pos2, gm, gv, w2, out
+):
+    nc = tc.nc
+    with ExitStack() as ctx:
+        keep = ctx.enter_context(tc.tile_pool(name="keep", bufs=1))
+        ring = ctx.enter_context(tc.tile_pool(name="ring", bufs=2))
+        psum = ctx.enter_context(tc.psum_pool(name="psum", bufs=1))
+
+        def bank(n, shape, name):
+            return psum.tile(shape, F32, tag="bank%d" % n, name=name)
+
+        offs_t = keep.tile([P, S // 16], U16, name="offs_t")
+        nc.sync.dma_start(offs_t[:], offs)
+        tabs = keep.tile([P, T], U8, name="tabs", tag="big2")
+        tv = tabs[:].bitcast(I32)
+        ts = tab_scales.bitcast(I32).rearrange("a (h e r) n -> e (a h) r n", h=2, e=2)
+        for e in range(2):
+            nc.sync.dma_start(tv[32 * e + 8 : 32 * e + 24, :], ts[e, 0:4])
+            nc.sync.dma_start(tv[32 * e + 24 : 32 * e + 32, :], ts[e, 4:6])
+        tab_src = [tab_words[a].rearrange("p t i -> p (t i)").bitcast(I32) for a in range(3)]
+        tabw = [keep.tile([P, T], I32, name="tabw%d" % a, tag="big%d" % a) for a in range(2)]
+        nc.sync.dma_start(tabw[0][:], tab_src[0])
+        w1sraw = keep.tile([P, 3, 256], I32, name="w1sraw")
+        nc.vector.memset(w1sraw[:], 0)
+        nc.vector.memset(tv[0:8, :], 0)
+        nc.vector.memset(tv[32:40, :], 0)
+        nc.vector.memset(tv[64:128, :], 0)
+
+        w1src = w1_words.bitcast(I32).rearrange("a p c -> p a c")
+        w1raw = [keep.tile([P, 3, 256], I32, name="w1raw0", tag="w1raw")]
+        nc.sync.dma_start(w1raw[0][:], w1src[:, :, 0:256])
+        pos = [keep.tile([P, M // 16], U16, name="pos%d" % s) for s in range(2)]
+        nc.sync.dma_start(pos[0][:], pos1)
+        nc.sync.dma_start(pos[1][:], pos2)
+        nc.sync.dma_start(tabw[1][:], tab_src[1])
+        w1ss = w1_scales.bitcast(I32)
+        for q in range(4):
+            nc.scalar.dma_start(
+                w1sraw[32 * q : 32 * q + 4, :, :], w1ss[:, 4 * q : 4 * q + 4, :].rearrange("a r n -> r a n")
+            )
+
+        warm = keep.tile([P, 1], F32, name="warm")
+        warm2 = keep.tile([P, 1], F32, name="warm2")
+        nc.vector.memset(warm[:], 0.0)
+        nc.scalar.activation(warm2[:], warm[:], ACT.Tanh)
+
+        gnat = keep.tile([4, 512], F32, name="gnat")
+        nc.gpsimd.dma_start(gnat[0:2, :], gm.rearrange("(b c) -> b c", b=2))
+        nc.gpsimd.dma_start(gnat[2:4, :], gv.rearrange("(b c) -> b c", b=2))
+        ident = keep.tile([P, P], F32, name="ident")
+        make_identity(nc, ident[:])
+        gord = keep.tile([P, 4, P], F32, name="gord")
+        nc.gpsimd.memset(gord[:], 0.0)
+        nc.scalar.copy(
+            gord[0:4].rearrange("p t (q i) -> p t q i", i=8), gnat[:].rearrange("p (q t i) -> p t q i", t=4, i=8)
+        )
+
+        vsg = keep.tile([P, S], U8, name="vsg")
+        nc.vector.tensor_copy(vsg[:], tabs[:].indirect(offs_t[:]))
+        tabw.append(keep.tile([P, T], I32, name="tabw2", tag="big2"))
+        nc.sync.dma_start(tabw[2][:], tab_src[2])
+        vs = [keep.tile([P, S], U8, name="vs%d" % a, align_bytes=64) for a in range(3)]
+        v0 = vsg[:].bitcast(I32)
+        for a in range(3):
+            va = vs[a][:].bitcast(I32)
+            for hf in range(2):
+                nc.scalar.dma_start(va[64 * hf : 64 * hf + 64, :], v0[8 + 8 * a + 4 * hf : 72 + 8 * a + 4 * hf, :])
+
+        w1w = [keep.tile([P, 3, 1024], U8, name="w1w%d" % b, tag="w1w%d" % b, align_bytes=64) for b in range(2)]
+        w1s = keep.tile([P, 3, 1024], U8, name="w1s", align_bytes=64)
+
+        def order_w1(b):
+            nc.vector.tensor_copy(
+                w1w[b][:].bitcast(I32).rearrange("p a (t q j) -> p a t q j", t=4, j=4),
+                w1raw[b][:].rearrange("p a (q t j) -> p a t q j", t=4, j=4),
+            )
+
+        order_w1(0)
+        nc.vector.tensor_copy(
+            w1s[:].bitcast(I32).rearrange("p a (b t q j) -> p (a b) t q j", b=2, t=4, j=2),
+            w1sraw[:].rearrange("p a (b q t j) -> p (a b) t q j", b=2, t=4, j=2),
+        )
+
+        vw = {}
+        for a in range(2):
+            g = keep.tile([P, S], U32, name="vw%d" % a, tag="vw%d" % a, align_bytes=64)
+            nc.vector.tensor_copy(g[:], tabw[a][:].bitcast(U32).indirect(offs_t[:]))
+            for hf in range(2):
+                vw[a, hf] = g[:, 512 * hf : 512 * hf + 512]
+        for hf in range(2):
+            g = keep.tile([P, 512], U32, name="vw2_%d" % hf, tag="vw2_%d" % hf, align_bytes=64)
+            nc.vector.tensor_copy(g[:], tabw[2][:].bitcast(U32).indirect(offs_t[:, 32 * hf : 32 * hf + 32]))
+            vw[2, hf] = g[:]
+
+        w1raw.append(keep.tile([P, 3, 256], I32, name="w1raw1", tag="w1raw"))
+        nc.sync.dma_start(w1raw[1][:], w1src[:, :, 256:512])
+        w2raw = [keep.tile([P, 4, H], F32, name="w2raw%d" % b, tag="big%d" % b) for b in range(2)]
+        w2v = w2.rearrange("(b q t i) n -> b t q i n", b=2, t=4, i=8)
+        for b in range(2):
+            for t in range(4):
+                nc.sync.dma_start(w2raw[b][:, t, :], w2v[b, t])
+        order_w1(1)
+
+        hs = [keep.tile([P, S], F32, name="h%d" % s) for s in range(8)]
+
+        def mm1(acc, s, hf, a):
+            b, t = divmod(s, 4)
+            nc.tensor.matmul_mx(
+                out=acc[:],
+                lhsT=w1w[b][:, a, 256 * t : 256 * t + 256].bitcast(FP4X4),
+                lhsT_scale=w1s[:, a, 128 * s : 128 * s + 128],
+                rhs=vw[a, hf].bitcast(FP8X4),
+                rhs_scale=vs[a][:, 512 * hf : 512 * hf + 512],
+                start=(a == 0),
+                stop=(a == 2),
+            )
+
+        accs = {(s, hf): bank(2 * s + hf, [P, 512], "acc%d_%d" % (s, hf)) for s in range(4) for hf in range(2)}
+        for a in range(2):
+            for s in range(4):
+                for hf in range(2):
+                    mm1(accs[s, hf], s, hf, a)
+        for s, hf in ((0, 0), (1, 0), (0, 1), (1, 1), (2, 0), (2, 1), (3, 0), (3, 1)):
+            if True:
+                mm1(accs[s, hf], s, hf, 2)
+                nc.scalar.copy(hs[s][:, 512 * hf : 512 * hf + 512], accs[s, hf][:])
+        gps = bank(0, [P, 4, P], "gps")
+        for t in range(4):
+            nc.tensor.transpose(gps[:, t, :], gord[:, t, :], ident[:])
+        gain = keep.tile([P, 4, 4], F32, name="gain")
+        nc.scalar.copy(gain[:], gps[:, :, 0:4].rearrange("p t j -> p j t"))
+        for s in range(4, 8):
+            for hf in range(2):
+                acc = bank(2 * (s - 4) + hf, [P, 512], "acc%d_%d" % (s, hf))
+                for a in range(3):
+                    mm1(acc, s, hf, a)
+                nc.scalar.copy(hs[s][:, 512 * hf : 512 * hf + 512], acc[:])
+
+        w2c = [keep.tile([P, H], U32, name="w2c%d" % b, align_bytes=64) for b in range(2)]
+        w2s = [keep.tile([P, H], U8, name="w2s%d" % b, align_bytes=64) for b in range(2)]
+
+        def quant_w2(b, nb, pool_engine):
+            wb = ring.tile([P, 512, 4], BF16, tag="wb", name="wb", align_bytes=64)
+            for tn in range(4):
+                if pool_engine:
+                    src = w2raw[b][:, :, 512 * nb : 512 * nb + 512].rearrange("p t (q u i) -> p u q i t", u=4, i=8)[:, tn]
+                    dst = wb[:, 128 * tn : 128 * tn + 128, :].rearrange("p (q i) t -> p q i t", i=8)
+                    nc.gpsimd.tensor_scalar(dst, src, 1.0, 0.0, MULT, mybir.AluOpType.add)
+                    continue
+                src = w2raw[b][:, :, 512 * nb : 512 * nb + 512].rearrange(
+                    "p t (q u h i) -> p u q h t i", u=4, h=2, i=4
+                )[:, tn]
+                dst = wb[:, 128 * tn : 128 * tn + 128, :].rearrange("p (q h i) t -> p q h t i", h=2, i=4)
+                nc.scalar.copy(dst, src)
+            nc.vector.quantize_mx(
+                out=w2c[b][:, 512 * nb : 512 * nb + 512].bitcast(FP8X4),
+                scales=w2s[b][:, 512 * nb : 512 * nb + 512],
+                in_=wb[:].rearrange("p m t -> p (m t)"),
+            )
+
+        zc = {}
+        zs = {}
+        picked = {}
+
+        def gather(side, b, c0, w, tag):
+            g = keep.tile([P, 4, w], F32, name="g%d_%d_%d" % (side, b, c0), tag=tag, align_bytes=64)
+            for t in range(4):
+                nc.vector.tensor_copy(
+                    g[:, t, :], hs[4 * b + t][:].indirect(pos[side][:, c0 // 16 : (c0 + w) // 16])
+                )
+            picked[side, b, c0] = g
+
+        def unit(side, b, c0, u0, w, eng):
+            g = picked[side, b, c0]
+            th = ring.tile([P, w, 4], F32, tag="th", name="th", bufs=3)
+            nc.scalar.activation(
+                th[:].rearrange("p (c i) t -> p c t i", i=4),
+                g[:, :, u0 - c0 : u0 - c0 + w].rearrange("p t (c i) -> p c t i", i=4),
+                ACT.Tanh,
+            )
+            zb = ring.tile([P, w, 4], BF16, tag="zb", name="zb", align_bytes=64, bufs=3)
+            j = 2 * side + b
+            eng.tensor_tensor(zb[:], th[:], gain[:, j : j + 1, :].to_broadcast([P, w, 4]), MULT)
+            c = keep.tile([P, w], U32, name="zc%d_%d_%d" % (side, b, u0), align_bytes=64)
+            sc = keep.tile([P, w], U8, name="zs%d_%d_%d" % (side, b, u0), align_bytes=64)
+            nc.vector.quantize_mx(out=c[:].bitcast(FP8X4), scales=sc[:], in_=zb[:].rearrange("p m t -> p (m t)"))
+            zc[side, b, u0] = c
+            zs[side, b, u0] = sc
+
+        def mm2(acc, s, side, b, c0, w, start, stop):
+            u0 = c0 if b == 1 else c0 - c0 % UNIT
+            nc.tensor.matmul_mx(
+                out=acc[:],
+                lhsT=w2c[b][:, 128 * s : 128 * s + 128].bitcast(FP8X4),
+                lhsT_scale=w2s[b][:, 128 * s : 128 * s + 128],
+                rhs=zc[side, b, u0][:, c0 - u0 : c0 - u0 + w].bitcast(FP8X4),
+                rhs_scale=zs[side, b, u0][:, c0 - u0 : c0 - u0 + w],
+                start=start,
+                stop=stop,
+            )
+
+        outv = out.rearrange("(b q t i) m -> b t q i m", b=2, t=4, i=8)
+
+        def second(c0, w):
+            ys = [bank(s, [P, w], "y%d_%d" % (s, c0)) for s in range(8)]
+            for n, (side, b) in enumerate(((0, 0), (1, 0), (0, 1))):
+                for s in range(8):
+                    mm2(ys[s], s, side, b, c0, w, n == 0, False)
+            for pair in range(4):
+                b, t0 = divmod(2 * pair, 4)
+                ay = ring.tile([P, 2, w], F32, tag="ay", name="ay", bufs=4)
+                for e in range(2):
+                    mm2(ys[2 * pair + e], 2 * pair + e, 1, 1, c0, w, False, True)
+                    nc.scalar.activation(ay[:, e, :], ys[2 * pair + e][:], ACT.Abs)
+                res = keep.tile([P, 2, w], F32, name="res%d_%d" % (pair, c0))
+                if b == 0:
+                    hv = picked[1, 0, 0][:, t0 : t0 + 2, c0 : c0 + w]
+                else:
+                    hv = picked[1, 1, c0][:, t0 : t0 + 2, :]
+                nc.vector.tensor_tensor(res[:], ay[:], hv, MULT)
+                for e in range(2):
+                    nc.sync.dma_start(outv[b, t0 + e][:, :, c0 : c0 + w], res[:, e, :])
+
+        gather(0, 0, 0, M, "gm0")
+        gather(1, 0, 0, M, "w1w0")
+        quant_w2(0, 0, True)
+        quant_w2(0, 1, True)
+        for side in range(2):
+            for u0 in range(0, M, UNIT):
+                unit(side, 0, 0, u0, UNIT, nc.gpsimd)
+        gather(0, 1, 0, 256, "gm1")
+        gather(1, 1, 0, 256, "gv1")
+        unit(0, 1, 0, 0, 256, nc.gpsimd)
+        unit(1, 1, 0, 0, 256, nc.vector)
+        quant_w2(1, 0, False)
+        quant_w2(1, 1, False)
+        gather(0, 1, 256, 128, "w1w1")
+        gather(1, 1, 256, 128, "vw0")
+        unit(0, 1, 256, 256, 128, nc.vector)
+        unit(1, 1, 256, 256, 128, nc.vector)
+        gather(0, 1, 384, 128, "vw1")
+        gather(1, 1, 384, 128, "vw2_1")
+        second(0, 256)
+        unit(0, 1, 384, 384, 128, nc.vector)
+        unit(1, 1, 384, 384, 128, nc.vector)
+        second(256, 128)
+        second(384, 128)

@@ -16,10 +16,15 @@ FP8X4 = mybir.dt.float8_e4m3fn_x4
 FP4X4 = mybir.dt.float4_e2m1fn_x4
 ACT = mybir.ActivationFunctionType
 MULT = mybir.AluOpType.mult
+ADD = mybir.AluOpType.add
 
 P = 128
-CHUNKS = [256,128,128]
-UNIT = 256
+PASSES = K // 512
+BANK = 512
+SLICES = H // P
+W = M // 2
+GAIN_RUN = 64
+MOUNTAIN, VALLEY = 0, 1
 
 
 def tile_list_crease_side_contrast_kernel(
@@ -36,237 +41,285 @@ def tile_list_crease_side_contrast_kernel(
 
         offs_t = keep.tile([P, S // 16], U16, name="offs_t")
         nc.sync.dma_start(offs_t[:], offs)
-        tabs = keep.tile([P, T], U8, name="tabs", tag="big2")
-        tv = tabs[:].bitcast(I32)
-        ts = tab_scales.bitcast(I32).rearrange("a (h e r) n -> e (a h) r n", h=2, e=2)
+
+        tab_s = keep.tile([P, T], U8, name="tab_s")
+        tab_s32 = tab_s[:].bitcast(I32)
+        tab_s_src = tab_scales.bitcast(I32).rearrange("a (u e c) n -> e (a u) c n", u=2, e=2)
         for e in range(2):
-            nc.sync.dma_start(tv[32 * e + 8 : 32 * e + 24, :], ts[e, 0:4])
-            nc.sync.dma_start(tv[32 * e + 24 : 32 * e + 32, :], ts[e, 4:6])
-        tab_src = [tab_words[a].rearrange("p t i -> p (t i)").bitcast(I32) for a in range(3)]
-        tabw = [keep.tile([P, T], I32, name="tabw%d" % a, tag="big%d" % a) for a in range(2)]
-        nc.sync.dma_start(tabw[0][:], tab_src[0])
-        w1sraw = keep.tile([P, 3, 256], I32, name="w1sraw")
-        nc.vector.memset(w1sraw[:], 0)
-        nc.vector.memset(tv[0:8, :], 0)
-        nc.vector.memset(tv[32:40, :], 0)
-        nc.vector.memset(tv[64:128, :], 0)
+            nc.sync.dma_start(tab_s32[32 * e + 8 : 32 * e + 24, :], tab_s_src[e, 0:4])
+            nc.sync.dma_start(tab_s32[32 * e + 24 : 32 * e + 32, :], tab_s_src[e, 4:6])
 
-        w1src = w1_words.bitcast(I32).rearrange("a p c -> p a c")
-        w1raw = [keep.tile([P, 3, 256], I32, name="w1raw0", tag="w1raw")]
-        nc.sync.dma_start(w1raw[0][:], w1src[:, :, 0:256])
-        pos = [keep.tile([P, M // 16], U16, name="pos%d" % s) for s in range(2)]
-        nc.sync.dma_start(pos[0][:], pos1)
-        nc.sync.dma_start(pos[1][:], pos2)
-        nc.sync.dma_start(tabw[1][:], tab_src[1])
-        w1ss = w1_scales.bitcast(I32)
-        for q in range(4):
+        zero = keep.tile([P, 1], F32, name="zero")
+        nc.vector.memset(zero[:], 0.0)
+        gain_rows = keep.tile([P, 4 * P], F32, name="gain_rows")
+        nc.scalar.activation(gain_rows[:], zero[:].to_broadcast([P, 4 * P]), ACT.Tanh)
+
+        tab_w_src = [tab_words[a].rearrange("p t i -> p (t i)").bitcast(I32) for a in range(PASSES)]
+        tab_w0 = keep.tile([P, T], I32, name="tab_w0", tag="tab_w0", align_bytes=64)
+        nc.sync.dma_start(tab_w0[:], tab_w_src[0])
+        w1_s_raw = keep.tile([P, PASSES, H // 4], I32, name="w1_s_raw", tag="w1_s_raw", align_bytes=64)
+        nc.vector.memset(tab_s32[0:8, :], 0)
+        nc.vector.memset(tab_s32[32:40, :], 0)
+        nc.vector.memset(tab_s32[64:128, :], 0)
+        nc.vector.memset(w1_s_raw[:], 0)
+
+        w1_w_src = w1_words.bitcast(I32).rearrange("a p c -> p a c")
+        w1_w_raw = [keep.tile([P, PASSES, BANK // 2], I32, name="w1_w_raw0", tag="w1_w_raw0", align_bytes=64)]
+        nc.sync.dma_start(w1_w_raw[0][:], w1_w_src[:, :, 0 : BANK // 2])
+        pos = [keep.tile([P, M // 16], U16, name="pos%d" % side) for side in (MOUNTAIN, VALLEY)]
+        nc.sync.dma_start(pos[MOUNTAIN][:], pos1)
+        nc.sync.dma_start(pos[VALLEY][:], pos2)
+        w1_s_src = w1_scales.bitcast(I32)
+        for quad in range(4):
             nc.scalar.dma_start(
-                w1sraw[32 * q : 32 * q + 4, :, :], w1ss[:, 4 * q : 4 * q + 4, :].rearrange("a r n -> r a n")
+                w1_s_raw[32 * quad : 32 * quad + 4, :, :],
+                w1_s_src[:, 4 * quad : 4 * quad + 4, :].rearrange("a c n -> c a n"),
             )
+        tab_w12 = keep.tile([P, 2 * T], I32, name="tab_w12", tag="tab_w12", align_bytes=64)
+        tab_w = [tab_w0[:], tab_w12[:, 0:T], tab_w12[:, T : 2 * T]]
+        nc.sync.dma_start(tab_w[1], tab_w_src[1])
+        nc.sync.dma_start(tab_w[2], tab_w_src[2])
 
-        warm = keep.tile([P, 1], F32, name="warm")
-        warm2 = keep.tile([P, 1], F32, name="warm2")
-        nc.vector.memset(warm[:], 0.0)
-        nc.scalar.activation(warm2[:], warm[:], ACT.Tanh)
-
-        gnat = keep.tile([4, 512], F32, name="gnat")
-        nc.gpsimd.dma_start(gnat[0:2, :], gm.rearrange("(b c) -> b c", b=2))
-        nc.gpsimd.dma_start(gnat[2:4, :], gv.rearrange("(b c) -> b c", b=2))
+        gain_raw = keep.tile([4, BANK], F32, name="gain_raw")
+        nc.gpsimd.dma_start(gain_raw[0:2, :], gm.rearrange("(b c) -> b c", b=2))
+        nc.gpsimd.dma_start(gain_raw[2:4, :], gv.rearrange("(b c) -> b c", b=2))
         ident = keep.tile([P, P], F32, name="ident")
         make_identity(nc, ident[:])
-        gord = keep.tile([P, 4, P], F32, name="gord")
-        nc.gpsimd.memset(gord[:], 0.0)
-        nc.scalar.copy(
-            gord[0:4].rearrange("p t (q i) -> p t q i", i=8), gnat[:].rearrange("p (q t i) -> p t q i", t=4, i=8)
-        )
 
-        vsg = keep.tile([P, S], U8, name="vsg")
-        nc.vector.tensor_copy(vsg[:], tabs[:].indirect(offs_t[:]))
-        tabw.append(keep.tile([P, T], I32, name="tabw2", tag="big2"))
-        nc.sync.dma_start(tabw[2][:], tab_src[2])
-        vs = [keep.tile([P, S], U8, name="vs%d" % a, align_bytes=64) for a in range(3)]
-        v0 = vsg[:].bitcast(I32)
-        for a in range(3):
-            va = vs[a][:].bitcast(I32)
-            for hf in range(2):
-                nc.scalar.dma_start(va[64 * hf : 64 * hf + 64, :], v0[8 + 8 * a + 4 * hf : 72 + 8 * a + 4 * hf, :])
+        v_s_all = keep.tile([P, S], U8, name="v_s_all", tag="v_s_all", align_bytes=64)
+        nc.vector.tensor_copy(v_s_all[:], tab_s[:].indirect(offs_t[:]))
+        v_s = [keep.tile([P, S], U8, name="v_s%d" % a, align_bytes=64) for a in range(PASSES)]
+        for a in range(PASSES):
+            for u in range(2):
+                first_row = 8 + 8 * a + 4 * u
+                nc.sync.dma_start(
+                    v_s[a][:].bitcast(I32)[64 * u : 64 * u + 64, :],
+                    v_s_all[:].bitcast(I32)[first_row : first_row + 64, :],
+                )
 
-        w1w = [keep.tile([P, 3, 1024], U8, name="w1w%d" % b, tag="w1w%d" % b, align_bytes=64) for b in range(2)]
-        w1s = keep.tile([P, 3, 1024], U8, name="w1s", align_bytes=64)
+        w1_w = [keep.tile([P, PASSES, 2 * BANK], U8, name="w1_w0", align_bytes=64)]
+        w1_s = keep.tile([P, PASSES, H], U8, name="w1_s", align_bytes=64)
 
-        def order_w1(b):
+        def order_w1_words(b):
             nc.vector.tensor_copy(
-                w1w[b][:].bitcast(I32).rearrange("p a (t q j) -> p a t q j", t=4, j=4),
-                w1raw[b][:].rearrange("p a (q t j) -> p a t q j", t=4, j=4),
+                w1_w[b][:].bitcast(I32).rearrange("p a (t q j) -> p a t q j", t=4, j=4),
+                w1_w_raw[b][:].rearrange("p a (q t j) -> p a t q j", t=4, j=4),
             )
 
-        order_w1(0)
+        order_w1_words(0)
         nc.vector.tensor_copy(
-            w1s[:].bitcast(I32).rearrange("p a (b t q j) -> p (a b) t q j", b=2, t=4, j=2),
-            w1sraw[:].rearrange("p a (b q t j) -> p (a b) t q j", b=2, t=4, j=2),
+            w1_s[:].bitcast(I32).rearrange("p a (b t q j) -> p (a b) t q j", b=2, t=4, j=2),
+            w1_s_raw[:].rearrange("p a (b q t j) -> p (a b) t q j", b=2, t=4, j=2),
         )
 
-        vw = {}
-        for a in range(2):
-            g = keep.tile([P, S], U32, name="vw%d" % a, tag="vw%d" % a, align_bytes=64)
-            nc.vector.tensor_copy(g[:], tabw[a][:].bitcast(U32).indirect(offs_t[:]))
-            for hf in range(2):
-                vw[a, hf] = g[:, 512 * hf : 512 * hf + 512]
-        for hf in range(2):
-            g = keep.tile([P, 512], U32, name="vw2_%d" % hf, tag="vw2_%d" % hf, align_bytes=64)
-            nc.vector.tensor_copy(g[:], tabw[2][:].bitcast(U32).indirect(offs_t[:, 32 * hf : 32 * hf + 32]))
-            vw[2, hf] = g[:]
+        v_w = {}
+        v_w_early = keep.tile([P, PASSES * BANK], U32, name="v_w_early", align_bytes=64)
+        v_w_late = keep.tile([P, PASSES * BANK], U32, name="v_w_late", tag="w1_s_raw", align_bytes=64)
+        for n in range(2 * PASSES):
+            a, half = divmod(n, 2)
+            place = BANK * (n % PASSES)
+            v_w[a, half] = (v_w_early if n < PASSES else v_w_late)[:, place : place + BANK]
+            nc.vector.tensor_copy(
+                v_w[a, half], tab_w[a].bitcast(U32).indirect(offs_t[:, 32 * half : 32 * half + 32])
+            )
 
-        w1raw.append(keep.tile([P, 3, 256], I32, name="w1raw1", tag="w1raw"))
-        nc.sync.dma_start(w1raw[1][:], w1src[:, :, 256:512])
-        w2raw = [keep.tile([P, 4, H], F32, name="w2raw%d" % b, tag="big%d" % b) for b in range(2)]
-        w2v = w2.rearrange("(b q t i) n -> b t q i n", b=2, t=4, i=8)
+        w1_w_raw.append(keep.tile([P, PASSES, BANK // 2], I32, name="w1_w_raw1", tag="tab_w0", align_bytes=64))
+        nc.sync.dma_start(w1_w_raw[1][:], w1_w_src[:, :, BANK // 2 : BANK])
+        w2_src = w2.rearrange("(b q t i) n -> b t q i n", b=2, t=4, i=8)
+        w2_raw00 = keep.tile([P, 4, BANK], F32, name="w2_raw00", tag="w1_w_raw0", align_bytes=64)
+        w2_raw01 = keep.tile([P, 4, BANK], F32, name="w2_raw01", tag="v_s_all", align_bytes=64)
+        w2_raw1 = keep.tile([P, 8, BANK], F32, name="w2_raw1", tag="tab_w12", align_bytes=64)
+        w2_raw = {(0, 0): w2_raw00[:], (0, 1): w2_raw01[:], (1, 0): w2_raw1[:, 0:4, :], (1, 1): w2_raw1[:, 4:8, :]}
         for b in range(2):
-            for t in range(4):
-                nc.sync.dma_start(w2raw[b][:, t, :], w2v[b, t])
-        order_w1(1)
+            for nb in range(2):
+                for t in range(4):
+                    nc.sync.dma_start(w2_raw[b, nb][:, t, :], w2_src[b, t][:, :, BANK * nb : BANK * nb + BANK])
 
-        hs = [keep.tile([P, S], F32, name="h%d" % s) for s in range(8)]
+        h = [keep.tile([P, S], F32, name="h%d" % s, tag="h%d" % s, align_bytes=64) for s in range(SLICES)]
 
-        def mm1(acc, s, hf, a):
+        def h_pass(acc, s, half, a):
             b, t = divmod(s, 4)
             nc.tensor.matmul_mx(
                 out=acc[:],
-                lhsT=w1w[b][:, a, 256 * t : 256 * t + 256].bitcast(FP4X4),
-                lhsT_scale=w1s[:, a, 128 * s : 128 * s + 128],
-                rhs=vw[a, hf].bitcast(FP8X4),
-                rhs_scale=vs[a][:, 512 * hf : 512 * hf + 512],
+                lhsT=w1_w[b][:, a, 2 * P * t : 2 * P * (t + 1)].bitcast(FP4X4),
+                lhsT_scale=w1_s[:, a, P * s : P * (s + 1)],
+                rhs=v_w[a, half].bitcast(FP8X4),
+                rhs_scale=v_s[a][:, BANK * half : BANK * (half + 1)],
                 start=(a == 0),
-                stop=(a == 2),
+                stop=(a == PASSES - 1),
             )
 
-        accs = {(s, hf): bank(2 * s + hf, [P, 512], "acc%d_%d" % (s, hf)) for s in range(4) for hf in range(2)}
-        for a in range(2):
-            for s in range(4):
-                for hf in range(2):
-                    mm1(accs[s, hf], s, hf, a)
-        for s, hf in ((0, 0), (1, 0), (0, 1), (1, 1), (2, 0), (2, 1), (3, 0), (3, 1)):
-            if True:
-                mm1(accs[s, hf], s, hf, 2)
-                nc.scalar.copy(hs[s][:, 512 * hf : 512 * hf + 512], accs[s, hf][:])
-        gps = bank(0, [P, 4, P], "gps")
-        for t in range(4):
-            nc.tensor.transpose(gps[:, t, :], gord[:, t, :], ident[:])
-        gain = keep.tile([P, 4, 4], F32, name="gain")
-        nc.scalar.copy(gain[:], gps[:, :, 0:4].rearrange("p t j -> p j t"))
-        for s in range(4, 8):
-            for hf in range(2):
-                acc = bank(2 * (s - 4) + hf, [P, 512], "acc%d_%d" % (s, hf))
-                for a in range(3):
-                    mm1(acc, s, hf, a)
-                nc.scalar.copy(hs[s][:, 512 * hf : 512 * hf + 512], acc[:])
+        def h_slice(s):
+            for half in range(2):
+                acc = bank(2 * (s % 4) + half, [P, BANK], "acc%d_%d" % (s, half))
+                for a in range(PASSES):
+                    h_pass(acc, s, half, a)
+                nc.scalar.copy(h[s][:, BANK * half : BANK * (half + 1)], acc[:])
 
-        w2c = [keep.tile([P, H], U32, name="w2c%d" % b, align_bytes=64) for b in range(2)]
-        w2s = [keep.tile([P, H], U8, name="w2s%d" % b, align_bytes=64) for b in range(2)]
+        w2_codes0 = keep.tile([P, H], U32, name="w2_codes0", tag="h%d" % (SLICES - 2), align_bytes=64)
+        codes = keep.tile([P, H + 8 * W], U32, name="codes", tag="h%d" % (SLICES - 1), align_bytes=64)
+        w2_c = [w2_codes0[:], codes[:, 0:H]]
+        w2_s = [keep.tile([P, H], U8, name="w2_s%d" % b, align_bytes=64) for b in range(2)]
 
-        def quant_w2(b, nb, pool_engine):
-            wb = ring.tile([P, 512, 4], BF16, tag="wb", name="wb", align_bytes=64)
+        def round_w2(b, nb):
+            wb = keep.tile([P, BANK, 4], BF16, tag="wb%d%d" % (b, nb), name="wb", align_bytes=64)
             for tn in range(4):
-                if pool_engine:
-                    src = w2raw[b][:, :, 512 * nb : 512 * nb + 512].rearrange("p t (q u i) -> p u q i t", u=4, i=8)[:, tn]
-                    dst = wb[:, 128 * tn : 128 * tn + 128, :].rearrange("p (q i) t -> p q i t", i=8)
-                    nc.gpsimd.tensor_scalar(dst, src, 1.0, 0.0, MULT, mybir.AluOpType.add)
-                    continue
-                src = w2raw[b][:, :, 512 * nb : 512 * nb + 512].rearrange(
-                    "p t (q u h i) -> p u q h t i", u=4, h=2, i=4
-                )[:, tn]
-                dst = wb[:, 128 * tn : 128 * tn + 128, :].rearrange("p (q h i) t -> p q h t i", h=2, i=4)
-                nc.scalar.copy(dst, src)
+                dst = wb[:, P * tn : P * (tn + 1), :]
+                if b == 0:
+                    nc.gpsimd.tensor_scalar(
+                        dst.rearrange("p (q i) t -> p q i t", i=8),
+                        w2_raw[b, nb].rearrange("p t (q tn i) -> p tn q i t", tn=4, i=8)[:, tn],
+                        1.0,
+                        0.0,
+                        MULT,
+                        ADD,
+                    )
+                else:
+                    nc.scalar.copy(
+                        dst.rearrange("p (q g j) t -> p q g t j", g=2, j=4),
+                        w2_raw[b, nb].rearrange("p t (q tn g j) -> p tn q g t j", tn=4, g=2, j=4)[:, tn],
+                    )
+            return wb
+
+        def quantise_w2(b, nb, wb):
             nc.vector.quantize_mx(
-                out=w2c[b][:, 512 * nb : 512 * nb + 512].bitcast(FP8X4),
-                scales=w2s[b][:, 512 * nb : 512 * nb + 512],
-                in_=wb[:].rearrange("p m t -> p (m t)"),
+                out=w2_c[b][:, BANK * nb : BANK * (nb + 1)].bitcast(FP8X4),
+                scales=w2_s[b][:, BANK * nb : BANK * (nb + 1)],
+                in_=wb[:].rearrange("p n t -> p (n t)"),
             )
 
-        zc = {}
-        zs = {}
-        picked = {}
+        picked = {
+            (side, b): keep.tile([P, 4, M], F32, name="picked%d_%d" % (side, b))
+            for side in (MOUNTAIN, VALLEY)
+            for b in range(2)
+        }
 
-        def gather(side, b, c0, w, tag):
-            g = keep.tile([P, 4, w], F32, name="g%d_%d_%d" % (side, b, c0), tag=tag, align_bytes=64)
-            for t in range(4):
-                nc.vector.tensor_copy(
-                    g[:, t, :], hs[4 * b + t][:].indirect(pos[side][:, c0 // 16 : (c0 + w) // 16])
-                )
-            picked[side, b, c0] = g
+        def pick(s):
+            b, t = divmod(s, 4)
+            for side in (MOUNTAIN, VALLEY):
+                nc.vector.tensor_copy(picked[side, b][:, t, :], h[s][:].indirect(pos[side][:]))
 
-        def unit(side, b, c0, u0, w, eng):
-            g = picked[side, b, c0]
-            th = ring.tile([P, w, 4], F32, tag="th", name="th", bufs=3)
+        def make_z(side, b, c0, th, z, engine):
             nc.scalar.activation(
-                th[:].rearrange("p (c i) t -> p c t i", i=4),
-                g[:, :, u0 - c0 : u0 - c0 + w].rearrange("p t (c i) -> p c t i", i=4),
+                th.rearrange("p (c j) t -> p c t j", j=4),
+                picked[side, b][:, :, c0 : c0 + W].rearrange("p t (c j) -> p c t j", j=4),
                 ACT.Tanh,
             )
-            zb = ring.tile([P, w, 4], BF16, tag="zb", name="zb", align_bytes=64, bufs=3)
-            j = 2 * side + b
-            eng.tensor_tensor(zb[:], th[:], gain[:, j : j + 1, :].to_broadcast([P, w, 4]), MULT)
-            c = keep.tile([P, w], U32, name="zc%d_%d_%d" % (side, b, u0), align_bytes=64)
-            sc = keep.tile([P, w], U8, name="zs%d_%d_%d" % (side, b, u0), align_bytes=64)
-            nc.vector.quantize_mx(out=c[:].bitcast(FP8X4), scales=sc[:], in_=zb[:].rearrange("p m t -> p (m t)"))
-            zc[side, b, u0] = c
-            zs[side, b, u0] = sc
-
-        def mm2(acc, s, side, b, c0, w, start, stop):
-            u0 = c0 if b == 1 else c0 - c0 % UNIT
-            nc.tensor.matmul_mx(
-                out=acc[:],
-                lhsT=w2c[b][:, 128 * s : 128 * s + 128].bitcast(FP8X4),
-                lhsT_scale=w2s[b][:, 128 * s : 128 * s + 128],
-                rhs=zc[side, b, u0][:, c0 - u0 : c0 - u0 + w].bitcast(FP8X4),
-                rhs_scale=zs[side, b, u0][:, c0 - u0 : c0 - u0 + w],
-                start=start,
-                stop=stop,
+            engine.tensor_tensor(
+                z[:].rearrange("p (g m) t -> p g (m t)", m=GAIN_RUN),
+                th.rearrange("p (g m) t -> p g (m t)", m=GAIN_RUN),
+                gain_run[2 * side + b][:]
+                .rearrange("p (g m) t -> p g (m t)", g=1)
+                .to_broadcast([P, W // GAIN_RUN, 4 * GAIN_RUN]),
+                MULT,
             )
 
-        outv = out.rearrange("(b q t i) m -> b t q i m", b=2, t=4, i=8)
+        z_c = {}
+        z_s = {}
 
-        def second(c0, w):
-            ys = [bank(s, [P, w], "y%d_%d" % (s, c0)) for s in range(8)]
-            for n, (side, b) in enumerate(((0, 0), (1, 0), (0, 1))):
-                for s in range(8):
-                    mm2(ys[s], s, side, b, c0, w, n == 0, False)
-            for pair in range(4):
+        def quantise_z(side, b, c0, z):
+            place = H + W * (4 * side + 2 * b + c0 // W)
+            z_c[side, b, c0] = codes[:, place : place + W]
+            z_s[side, b, c0] = keep.tile([P, W], U8, name="z_s%d_%d_%d" % (side, b, c0), align_bytes=64)
+            nc.vector.quantize_mx(
+                out=z_c[side, b, c0].bitcast(FP8X4), scales=z_s[side, b, c0][:], in_=z[:].rearrange("p m t -> p (m t)")
+            )
+
+        def z_of_pass_1(side, c0):
+            th = ring.tile([P, W, 4], F32, tag="th", name="th", bufs=4)
+            z = ring.tile([P, W, 4], BF16, tag="z", name="z", align_bytes=64, bufs=3)
+            make_z(side, 1, c0, th[:], z, nc.vector)
+            quantise_z(side, 1, c0, z)
+
+        y = {}
+
+        def y_passes(c0, side, b):
+            for pair in range(SLICES // 2):
+                if (c0, pair) not in y:
+                    y[c0, pair] = bank(4 * (c0 // W) + pair, [P, 2, W], "y%d_%d" % (c0, pair))
+                for e in range(2):
+                    s = 2 * pair + e
+                    nc.tensor.matmul_mx(
+                        out=y[c0, pair][:, e, :],
+                        lhsT=w2_c[b][:, P * s : P * (s + 1)].bitcast(FP8X4),
+                        lhsT_scale=w2_s[b][:, P * s : P * (s + 1)],
+                        rhs=z_c[side, b, c0].bitcast(FP8X4),
+                        rhs_scale=z_s[side, b, c0][:],
+                        start=(side == MOUNTAIN and b == 0 and e == 0),
+                        stop=(side == VALLEY and b == 1 and e == 1),
+                    )
+
+        out_rows = out.rearrange("(b q t i) m -> b t q i m", b=2, t=4, i=8)
+
+        def finish(c0):
+            for pair in range(SLICES // 2):
                 b, t0 = divmod(2 * pair, 4)
-                ay = ring.tile([P, 2, w], F32, tag="ay", name="ay", bufs=4)
+                y_abs = ring.tile([P, 2, W], F32, tag="y_abs", name="y_abs", bufs=SLICES // 2)
+                nc.scalar.activation(y_abs[:], y[c0, pair][:], ACT.Abs)
+                res = keep.tile([P, 2, W], F32, name="res%d_%d" % (pair, c0))
+                nc.vector.tensor_tensor(res[:], y_abs[:], picked[VALLEY, b][:, t0 : t0 + 2, c0 : c0 + W], MULT)
                 for e in range(2):
-                    mm2(ys[2 * pair + e], 2 * pair + e, 1, 1, c0, w, False, True)
-                    nc.scalar.activation(ay[:, e, :], ys[2 * pair + e][:], ACT.Abs)
-                res = keep.tile([P, 2, w], F32, name="res%d_%d" % (pair, c0))
-                if b == 0:
-                    hv = picked[1, 0, 0][:, t0 : t0 + 2, c0 : c0 + w]
-                else:
-                    hv = picked[1, 1, c0][:, t0 : t0 + 2, :]
-                nc.vector.tensor_tensor(res[:], ay[:], hv, MULT)
-                for e in range(2):
-                    nc.sync.dma_start(outv[b, t0 + e][:, :, c0 : c0 + w], res[:, e, :])
+                    nc.sync.dma_start(out_rows[b, t0 + e][:, :, c0 : c0 + W], res[:, e, :])
 
-        gather(0, 0, 0, M, "gm0")
-        gather(1, 0, 0, M, "w1w0")
-        quant_w2(0, 0, True)
-        quant_w2(0, 1, True)
-        for side in range(2):
-            for u0 in range(0, M, UNIT):
-                unit(side, 0, 0, u0, UNIT, nc.gpsimd)
-        gather(0, 1, 0, 256, "gm1")
-        gather(1, 1, 0, 256, "gv1")
-        unit(0, 1, 0, 0, 256, nc.gpsimd)
-        unit(1, 1, 0, 0, 256, nc.vector)
-        quant_w2(1, 0, False)
-        quant_w2(1, 1, False)
-        gather(0, 1, 256, 128, "w1w1")
-        gather(1, 1, 256, 128, "vw0")
-        unit(0, 1, 256, 256, 128, nc.vector)
-        unit(1, 1, 256, 256, 128, nc.vector)
-        gather(0, 1, 384, 128, "vw1")
-        gather(1, 1, 384, 128, "vw2_1")
-        second(0, 256)
-        unit(0, 1, 384, 384, 128, nc.vector)
-        unit(1, 1, 384, 384, 128, nc.vector)
-        second(256, 128)
-        second(384, 128)
+        acc0 = [bank(half, [P, BANK], "acc0_%d" % half) for half in range(2)]
+        for a in range(PASSES - 1):
+            for half in range(2):
+                h_pass(acc0[half], 0, half, a)
+        for half in range(2):
+            h_pass(acc0[half], 0, half, PASSES - 1)
+            nc.scalar.copy(h[0][:, BANK * half : BANK * (half + 1)], acc0[half][:])
+        w1_w.append(keep.tile([P, PASSES, 2 * BANK], U8, name="w1_w1", align_bytes=64))
+        order_w1_words(1)
+        h_slice(1)
+
+        gain_by_t = gain_rows[:].rearrange("p (t c) -> p t c", t=4)
+        nc.gpsimd.tensor_copy(
+            gain_by_t[0:4].rearrange("p t (q i) -> p t q i", i=8),
+            gain_raw[:].rearrange("p (q t i) -> p t q i", t=4, i=8),
+        )
+        gain_ps = bank(7, [P, 4, P], "gain_ps")
+        for t in range(4):
+            nc.tensor.transpose(gain_ps[:, t, :], gain_by_t[:, t, :], ident[:])
+        gain = keep.tile([P, 4, 4], F32, name="gain")
+        nc.scalar.copy(gain[:], gain_ps[:, :, 0:4].rearrange("p t j -> p j t"))
+        gain_run = [keep.tile([P, GAIN_RUN, 4], F32, name="gain_run%d" % j) for j in range(4)]
+        for j in range(4):
+            nc.scalar.copy(gain_run[j][:], gain[:, j : j + 1, :].to_broadcast([P, GAIN_RUN, 4]))
+
+        for s in range(2, SLICES):
+            h_slice(s)
+        for s in range(SLICES - 1):
+            pick(s)
+        wb0 = [round_w2(0, nb) for nb in range(2)]
+        for nb in range(2):
+            quantise_w2(0, nb, wb0[nb])
+        pick(SLICES - 1)
+
+        th0 = keep.tile([P, 4, W, 4], F32, name="th0", tag="v_s_all", align_bytes=64)
+        pieces = [(MOUNTAIN, 0), (MOUNTAIN, W), (VALLEY, 0), (VALLEY, W)]
+        z0 = {}
+        for n, (side, c0) in enumerate(pieces):
+            tag = "wb01" if (side, c0) == (VALLEY, 0) else "z0_%d" % n
+            z0[side, c0] = keep.tile([P, W, 4], BF16, tag=tag, name="z0", align_bytes=64)
+            make_z(side, 0, c0, th0[:, n], z0[side, c0], nc.vector if n == len(pieces) - 1 else nc.gpsimd)
+        wb1 = [round_w2(1, nb) for nb in range(2)]
+        for side, c0 in pieces[:-1]:
+            quantise_z(side, 0, c0, z0[side, c0])
+        y_passes(0, MOUNTAIN, 0)
+        y_passes(0, VALLEY, 0)
+        for nb in range(2):
+            quantise_w2(1, nb, wb1[nb])
+        quantise_z(VALLEY, 0, W, z0[VALLEY, W])
+
+        z_of_pass_1(MOUNTAIN, 0)
+        z_of_pass_1(VALLEY, 0)
+        y_passes(0, MOUNTAIN, 1)
+        y_passes(0, VALLEY, 1)
+        y_passes(W, MOUNTAIN, 0)
+        y_passes(W, VALLEY, 0)
+        z_of_pass_1(MOUNTAIN, W)
+        z_of_pass_1(VALLEY, W)
+        finish(0)
+        y_passes(W, MOUNTAIN, 1)
+        y_passes(W, VALLEY, 1)
+        finish(W)

from contextlib import ExitStack

import concourse.mybir as mybir
from concourse.masks import make_identity

K, H, T, S, M = 1536, 1024, 2048, 1024, 512
FLOPS = 2 * K * H * S + 2 * 2 * H * H * M

F32 = mybir.dt.float32
BF16 = mybir.dt.bfloat16
I32 = mybir.dt.int32
U32 = mybir.dt.uint32
U16 = mybir.dt.uint16
U8 = mybir.dt.uint8
FP8X4 = mybir.dt.float8_e4m3fn_x4
FP4X4 = mybir.dt.float4_e2m1fn_x4
ACT = mybir.ActivationFunctionType
MULT = mybir.AluOpType.mult
ADD = mybir.AluOpType.add

P = 128
PASSES = K // 512
BANK = 512
SLICES = H // P
W = M // 2
GAIN_RUN = 64
MOUNTAIN, VALLEY = 0, 1


def tile_list_crease_side_contrast_kernel(
    tc, tab_words, tab_scales, offs, w1_words, w1_scales, pos1, pos2, gm, gv, w2, out
):
    nc = tc.nc
    with ExitStack() as ctx:
        keep = ctx.enter_context(tc.tile_pool(name="keep", bufs=1))
        ring = ctx.enter_context(tc.tile_pool(name="ring", bufs=2))
        psum = ctx.enter_context(tc.psum_pool(name="psum", bufs=1))

        def bank(n, shape, name):
            return psum.tile(shape, F32, tag="bank%d" % n, name=name)

        offs_t = keep.tile([P, S // 16], U16, name="offs_t")
        nc.sync.dma_start(offs_t[:], offs)

        tab_s = keep.tile([P, T], U8, name="tab_s")
        tab_s32 = tab_s[:].bitcast(I32)
        tab_s_src = tab_scales.bitcast(I32).rearrange("a (u e c) n -> e (a u) c n", u=2, e=2)
        for e in range(2):
            nc.sync.dma_start(tab_s32[32 * e + 8 : 32 * e + 24, :], tab_s_src[e, 0:4])
            nc.sync.dma_start(tab_s32[32 * e + 24 : 32 * e + 32, :], tab_s_src[e, 4:6])

        zero = keep.tile([P, 1], F32, name="zero")
        nc.vector.memset(zero[:], 0.0)
        gain_rows = keep.tile([P, 4 * P], F32, name="gain_rows")
        nc.scalar.activation(gain_rows[:], zero[:].to_broadcast([P, 4 * P]), ACT.Tanh)

        tab_w_src = [tab_words[a].rearrange("p t i -> p (t i)").bitcast(I32) for a in range(PASSES)]
        tab_w0 = keep.tile([P, T], I32, name="tab_w0", tag="tab_w0", align_bytes=64)
        nc.sync.dma_start(tab_w0[:], tab_w_src[0])
        w1_s_raw = keep.tile([P, PASSES, H // 4], I32, name="w1_s_raw", tag="w1_s_raw", align_bytes=64)
        nc.vector.memset(tab_s32[0:8, :], 0)
        nc.vector.memset(tab_s32[32:40, :], 0)
        nc.vector.memset(tab_s32[64:128, :], 0)
        nc.vector.memset(w1_s_raw[:], 0)

        w1_w_src = w1_words.bitcast(I32).rearrange("a p c -> p a c")
        w1_w_raw = [keep.tile([P, PASSES, BANK // 2], I32, name="w1_w_raw0", tag="w1_w_raw0", align_bytes=64)]
        nc.sync.dma_start(w1_w_raw[0][:], w1_w_src[:, :, 0 : BANK // 2])
        pos = [keep.tile([P, M // 16], U16, name="pos%d" % side) for side in (MOUNTAIN, VALLEY)]
        nc.sync.dma_start(pos[MOUNTAIN][:], pos1)
        nc.sync.dma_start(pos[VALLEY][:], pos2)
        w1_s_src = w1_scales.bitcast(I32)
        for quad in range(4):
            nc.scalar.dma_start(
                w1_s_raw[32 * quad : 32 * quad + 4, :, :],
                w1_s_src[:, 4 * quad : 4 * quad + 4, :].rearrange("a c n -> c a n"),
            )
        tab_w12 = keep.tile([P, 2 * T], I32, name="tab_w12", tag="tab_w12", align_bytes=64)
        tab_w = [tab_w0[:], tab_w12[:, 0:T], tab_w12[:, T : 2 * T]]
        nc.sync.dma_start(tab_w[1], tab_w_src[1])
        nc.sync.dma_start(tab_w[2], tab_w_src[2])

        gain_raw = keep.tile([4, BANK], F32, name="gain_raw")
        nc.gpsimd.dma_start(gain_raw[0:2, :], gm.rearrange("(b c) -> b c", b=2))
        nc.gpsimd.dma_start(gain_raw[2:4, :], gv.rearrange("(b c) -> b c", b=2))
        ident = keep.tile([P, P], F32, name="ident")
        make_identity(nc, ident[:])

        v_s_all = keep.tile([P, S], U8, name="v_s_all", tag="v_s_all", align_bytes=64)
        nc.vector.tensor_copy(v_s_all[:], tab_s[:].indirect(offs_t[:]))
        v_s = [keep.tile([P, S], U8, name="v_s%d" % a, align_bytes=64) for a in range(PASSES)]
        for a in range(PASSES):
            for u in range(2):
                first_row = 8 + 8 * a + 4 * u
                nc.sync.dma_start(
                    v_s[a][:].bitcast(I32)[64 * u : 64 * u + 64, :],
                    v_s_all[:].bitcast(I32)[first_row : first_row + 64, :],
                )

        w1_w = [keep.tile([P, PASSES, 2 * BANK], U8, name="w1_w0", align_bytes=64)]
        w1_s = keep.tile([P, PASSES, H], U8, name="w1_s", align_bytes=64)

        def order_w1_words(b):
            nc.vector.tensor_copy(
                w1_w[b][:].bitcast(I32).rearrange("p a (t q j) -> p a t q j", t=4, j=4),
                w1_w_raw[b][:].rearrange("p a (q t j) -> p a t q j", t=4, j=4),
            )

        order_w1_words(0)
        nc.vector.tensor_copy(
            w1_s[:].bitcast(I32).rearrange("p a (b t q j) -> p (a b) t q j", b=2, t=4, j=2),
            w1_s_raw[:].rearrange("p a (b q t j) -> p (a b) t q j", b=2, t=4, j=2),
        )

        v_w = {}
        v_w_early = keep.tile([P, PASSES * BANK], U32, name="v_w_early", align_bytes=64)
        v_w_late = keep.tile([P, PASSES * BANK], U32, name="v_w_late", tag="w1_s_raw", align_bytes=64)
        for n in range(2 * PASSES):
            a, half = divmod(n, 2)
            place = BANK * (n % PASSES)
            v_w[a, half] = (v_w_early if n < PASSES else v_w_late)[:, place : place + BANK]
            nc.vector.tensor_copy(
                v_w[a, half], tab_w[a].bitcast(U32).indirect(offs_t[:, 32 * half : 32 * half + 32])
            )

        w1_w_raw.append(keep.tile([P, PASSES, BANK // 2], I32, name="w1_w_raw1", tag="tab_w0", align_bytes=64))
        nc.sync.dma_start(w1_w_raw[1][:], w1_w_src[:, :, BANK // 2 : BANK])
        w2_src = w2.rearrange("(b q t i) n -> b t q i n", b=2, t=4, i=8)
        w2_raw00 = keep.tile([P, 4, BANK], F32, name="w2_raw00", tag="w1_w_raw0", align_bytes=64)
        w2_raw01 = keep.tile([P, 4, BANK], F32, name="w2_raw01", tag="v_s_all", align_bytes=64)
        w2_raw1 = keep.tile([P, 8, BANK], F32, name="w2_raw1", tag="tab_w12", align_bytes=64)
        w2_raw = {(0, 0): w2_raw00[:], (0, 1): w2_raw01[:], (1, 0): w2_raw1[:, 0:4, :], (1, 1): w2_raw1[:, 4:8, :]}
        for b in range(2):
            for nb in range(2):
                for t in range(4):
                    nc.sync.dma_start(w2_raw[b, nb][:, t, :], w2_src[b, t][:, :, BANK * nb : BANK * nb + BANK])

        h = [keep.tile([P, S], F32, name="h%d" % s, tag="h%d" % s, align_bytes=64) for s in range(SLICES)]

        def h_pass(acc, s, half, a):
            b, t = divmod(s, 4)
            nc.tensor.matmul_mx(
                out=acc[:],
                lhsT=w1_w[b][:, a, 2 * P * t : 2 * P * (t + 1)].bitcast(FP4X4),
                lhsT_scale=w1_s[:, a, P * s : P * (s + 1)],
                rhs=v_w[a, half].bitcast(FP8X4),
                rhs_scale=v_s[a][:, BANK * half : BANK * (half + 1)],
                start=(a == 0),
                stop=(a == PASSES - 1),
            )

        def h_slice(s):
            for half in range(2):
                acc = bank(2 * (s % 4) + half, [P, BANK], "acc%d_%d" % (s, half))
                for a in range(PASSES):
                    h_pass(acc, s, half, a)
                nc.scalar.copy(h[s][:, BANK * half : BANK * (half + 1)], acc[:])

        w2_codes0 = keep.tile([P, H], U32, name="w2_codes0", tag="h%d" % (SLICES - 2), align_bytes=64)
        codes = keep.tile([P, H + 8 * W], U32, name="codes", tag="h%d" % (SLICES - 1), align_bytes=64)
        w2_c = [w2_codes0[:], codes[:, 0:H]]
        w2_s = [keep.tile([P, H], U8, name="w2_s%d" % b, align_bytes=64) for b in range(2)]

        def round_w2(b, nb):
            wb = keep.tile([P, BANK, 4], BF16, tag="wb%d%d" % (b, nb), name="wb", align_bytes=64)
            for tn in range(4):
                dst = wb[:, P * tn : P * (tn + 1), :]
                if b == 0:
                    nc.gpsimd.tensor_scalar(
                        dst.rearrange("p (q i) t -> p q i t", i=8),
                        w2_raw[b, nb].rearrange("p t (q tn i) -> p tn q i t", tn=4, i=8)[:, tn],
                        1.0,
                        0.0,
                        MULT,
                        ADD,
                    )
                else:
                    nc.scalar.copy(
                        dst.rearrange("p (q g j) t -> p q g t j", g=2, j=4),
                        w2_raw[b, nb].rearrange("p t (q tn g j) -> p tn q g t j", tn=4, g=2, j=4)[:, tn],
                    )
            return wb

        def quantise_w2(b, nb, wb):
            nc.vector.quantize_mx(
                out=w2_c[b][:, BANK * nb : BANK * (nb + 1)].bitcast(FP8X4),
                scales=w2_s[b][:, BANK * nb : BANK * (nb + 1)],
                in_=wb[:].rearrange("p n t -> p (n t)"),
            )

        picked = {
            (side, b): keep.tile([P, 4, M], F32, name="picked%d_%d" % (side, b))
            for side in (MOUNTAIN, VALLEY)
            for b in range(2)
        }

        def pick(s):
            b, t = divmod(s, 4)
            for side in (MOUNTAIN, VALLEY):
                nc.vector.tensor_copy(picked[side, b][:, t, :], h[s][:].indirect(pos[side][:]))

        def make_z(side, b, c0, th, z, engine):
            nc.scalar.activation(
                th.rearrange("p (c j) t -> p c t j", j=4),
                picked[side, b][:, :, c0 : c0 + W].rearrange("p t (c j) -> p c t j", j=4),
                ACT.Tanh,
            )
            engine.tensor_tensor(
                z[:].rearrange("p (g m) t -> p g (m t)", m=GAIN_RUN),
                th.rearrange("p (g m) t -> p g (m t)", m=GAIN_RUN),
                gain_run[2 * side + b][:]
                .rearrange("p (g m) t -> p g (m t)", g=1)
                .to_broadcast([P, W // GAIN_RUN, 4 * GAIN_RUN]),
                MULT,
            )

        z_c = {}
        z_s = {}

        def quantise_z(side, b, c0, z):
            place = H + W * (4 * side + 2 * b + c0 // W)
            z_c[side, b, c0] = codes[:, place : place + W]
            z_s[side, b, c0] = keep.tile([P, W], U8, name="z_s%d_%d_%d" % (side, b, c0), align_bytes=64)
            nc.vector.quantize_mx(
                out=z_c[side, b, c0].bitcast(FP8X4), scales=z_s[side, b, c0][:], in_=z[:].rearrange("p m t -> p (m t)")
            )

        def z_of_pass_1(side, c0):
            th = ring.tile([P, W, 4], F32, tag="th", name="th", bufs=4)
            z = ring.tile([P, W, 4], BF16, tag="z", name="z", align_bytes=64, bufs=3)
            make_z(side, 1, c0, th[:], z, nc.vector)
            quantise_z(side, 1, c0, z)

        y = {}

        def y_passes(c0, side, b):
            for pair in range(SLICES // 2):
                if (c0, pair) not in y:
                    y[c0, pair] = bank(4 * (c0 // W) + pair, [P, 2, W], "y%d_%d" % (c0, pair))
                for e in range(2):
                    s = 2 * pair + e
                    nc.tensor.matmul_mx(
                        out=y[c0, pair][:, e, :],
                        lhsT=w2_c[b][:, P * s : P * (s + 1)].bitcast(FP8X4),
                        lhsT_scale=w2_s[b][:, P * s : P * (s + 1)],
                        rhs=z_c[side, b, c0].bitcast(FP8X4),
                        rhs_scale=z_s[side, b, c0][:],
                        start=(side == MOUNTAIN and b == 0 and e == 0),
                        stop=(side == VALLEY and b == 1 and e == 1),
                    )

        out_rows = out.rearrange("(b q t i) m -> b t q i m", b=2, t=4, i=8)

        def finish(c0):
            for pair in range(SLICES // 2):
                b, t0 = divmod(2 * pair, 4)
                y_abs = ring.tile([P, 2, W], F32, tag="y_abs", name="y_abs", bufs=SLICES // 2)
                nc.scalar.activation(y_abs[:], y[c0, pair][:], ACT.Abs)
                res = keep.tile([P, 2, W], F32, name="res%d_%d" % (pair, c0))
                nc.vector.tensor_tensor(res[:], y_abs[:], picked[VALLEY, b][:, t0 : t0 + 2, c0 : c0 + W], MULT)
                for e in range(2):
                    nc.sync.dma_start(out_rows[b, t0 + e][:, :, c0 : c0 + W], res[:, e, :])

        acc0 = [bank(half, [P, BANK], "acc0_%d" % half) for half in range(2)]
        for a in range(PASSES - 1):
            for half in range(2):
                h_pass(acc0[half], 0, half, a)
        for half in range(2):
            h_pass(acc0[half], 0, half, PASSES - 1)
            nc.scalar.copy(h[0][:, BANK * half : BANK * (half + 1)], acc0[half][:])
        w1_w.append(keep.tile([P, PASSES, 2 * BANK], U8, name="w1_w1", align_bytes=64))
        order_w1_words(1)
        h_slice(1)

        gain_by_t = gain_rows[:].rearrange("p (t c) -> p t c", t=4)
        nc.gpsimd.tensor_copy(
            gain_by_t[0:4].rearrange("p t (q i) -> p t q i", i=8),
            gain_raw[:].rearrange("p (q t i) -> p t q i", t=4, i=8),
        )
        gain_ps = bank(7, [P, 4, P], "gain_ps")
        for t in range(4):
            nc.tensor.transpose(gain_ps[:, t, :], gain_by_t[:, t, :], ident[:])
        gain = keep.tile([P, 4, 4], F32, name="gain")
        nc.scalar.copy(gain[:], gain_ps[:, :, 0:4].rearrange("p t j -> p j t"))
        gain_run = [keep.tile([P, GAIN_RUN, 4], F32, name="gain_run%d" % j) for j in range(4)]
        for j in range(4):
            nc.scalar.copy(gain_run[j][:], gain[:, j : j + 1, :].to_broadcast([P, GAIN_RUN, 4]))

        for s in range(2, SLICES):
            h_slice(s)
        for s in range(SLICES - 1):
            pick(s)
        wb0 = [round_w2(0, nb) for nb in range(2)]
        for nb in range(2):
            quantise_w2(0, nb, wb0[nb])
        pick(SLICES - 1)

        th0 = keep.tile([P, 4, W, 4], F32, name="th0", tag="v_s_all", align_bytes=64)
        pieces = [(MOUNTAIN, 0), (MOUNTAIN, W), (VALLEY, 0), (VALLEY, W)]
        z0 = {}
        for n, (side, c0) in enumerate(pieces):
            tag = "wb01" if (side, c0) == (VALLEY, 0) else "z0_%d" % n
            z0[side, c0] = keep.tile([P, W, 4], BF16, tag=tag, name="z0", align_bytes=64)
            make_z(side, 0, c0, th0[:, n], z0[side, c0], nc.vector if n == len(pieces) - 1 else nc.gpsimd)
        wb1 = [round_w2(1, nb) for nb in range(2)]
        for side, c0 in pieces[:-1]:
            quantise_z(side, 0, c0, z0[side, c0])
        y_passes(0, MOUNTAIN, 0)
        y_passes(0, VALLEY, 0)
        for nb in range(2):
            quantise_w2(1, nb, wb1[nb])
        quantise_z(VALLEY, 0, W, z0[VALLEY, W])

        z_of_pass_1(MOUNTAIN, 0)
        z_of_pass_1(VALLEY, 0)
        y_passes(0, MOUNTAIN, 1)
        y_passes(0, VALLEY, 1)
        y_passes(W, MOUNTAIN, 0)
        y_passes(W, VALLEY, 0)
        z_of_pass_1(MOUNTAIN, W)
        z_of_pass_1(VALLEY, W)
        finish(0)
        y_passes(W, MOUNTAIN, 1)
        y_passes(W, VALLEY, 1)
        finish(W)
